import numpy as np
import ml_dtypes


def mxq(x, axis, fmt="e4m3"):
    dtype, down = {"e4m3": (ml_dtypes.float8_e4m3fn, 7), "e5m2": (ml_dtypes.float8_e5m2, 14)}[fmt]
    v = np.moveaxis(np.asarray(x, np.float32).astype(ml_dtypes.bfloat16).astype(np.float64), axis, -1)
    blocks = v.reshape(v.shape[:-1] + (-1, 32))
    amax = np.abs(blocks).max(-1, keepdims=True)
    byte = np.maximum(np.where(amax > 0, np.frexp(amax)[1] - 1 + 127, 0) - down, 1)
    scale = np.exp2(byte - 127.0)
    codes = (blocks / scale).astype(np.float32).astype(dtype).astype(np.float64)
    return np.moveaxis((codes * scale).reshape(v.shape), -1, axis)


WIDE = False


def mx_kscale(k):
    if not WIDE:
        return np.ones(k)
    levels = np.array([10, -10, 5, -5, 0])
    if k % 512:
        return np.exp2(np.random.permutation(np.resize(levels, k // 32))).repeat(32)
    a = np.empty((k // 512, 16))
    for p in range(k // 512):
        a[p, :8] = np.random.permutation(np.resize(levels, 8))
        for g in range(8):
            far = levels[np.abs(levels - a[p, g]) >= 10]
            a[p, g + 8] = far[np.random.randint(len(far))]
    return np.exp2(a.ravel()).repeat(32)


def f64(x):
    return np.asarray(x).astype(np.float64)


def striped(idx):
    return np.tile(idx.reshape(-1, 16).T, (8, 1)).astype(np.uint16)


def unstriped(offs):
    return offs[:16].T.reshape(-1).astype(np.int64)


E2M1 = np.array([0.0, 0.5, 1.0, 1.5, 2.0, 3.0, 4.0, 6.0, -0.0, -0.5, -1.0, -1.5, -2.0, -3.0, -4.0, -6.0])


def pack_weight(w, fmt):
    k, n = w.shape
    w = f64(np.asarray(w, np.float32).astype(ml_dtypes.bfloat16)).reshape(k // 32, 32, n)
    amax = np.abs(w).max(1)
    if fmt == "e4m3":
        byte = np.frexp(amax)[1] - 1 + 127 - 7
    else:
        mant, ex = np.frexp(amax / 6.0)
        byte = np.where(mant > 0.5, ex, ex - 1) + 127
    byte = np.clip(np.where(amax > 0, byte, 1), 1, 254)
    scaled = (w * np.exp2(127.0 - byte)[:, None, :]).reshape(k, n).astype(np.float32)
    by_word = np.ascontiguousarray(scaled.reshape(k // 512, 128, 4, n).transpose(0, 1, 3, 2))
    if fmt == "e4m3":
        words = by_word.astype(ml_dtypes.float8_e4m3fn).view(np.uint8)
    else:
        c = by_word.astype(ml_dtypes.float4_e2m1fn).view(np.uint8) & 0xF
        words = (c[..., 0::2] | (c[..., 1::2] << 4)).reshape(k // 512, 128, 2 * n)
    return np.ascontiguousarray(words), np.ascontiguousarray(byte.astype(np.uint8).reshape(k // 512, 16, n))


def unpack_weight(words, scales, fmt):
    g, _, n = scales.shape
    words = np.ascontiguousarray(words).reshape(g, 128, n, -1)
    if fmt == "e4m3":
        vals = words.view(ml_dtypes.float8_e4m3fn).astype(np.float64)
    else:
        nib = np.empty((g, 128, n, 4), np.uint8)
        nib[..., 0::2] = words & 0xF
        nib[..., 1::2] = words >> 4
        vals = E2M1[nib]
    vals = vals * np.repeat(np.exp2(scales.astype(np.float64) - 127.0), 8, axis=1)[..., None]
    return vals.transpose(0, 1, 3, 2).reshape(g * 512, n)


def gelu(v):
    return 0.5 * v * (1.0 + np.tanh(np.sqrt(2.0 / np.pi) * (v + 0.044715 * v**3)))


def bf(x):
    return np.asarray(x, np.float32).astype(ml_dtypes.bfloat16)


def planes(Y):
    n, m = Y.shape
    b = f64(bf(Y)).reshape(n // 32, 32, m)
    amax = np.abs(b).max(1)
    byte = np.clip(np.where(amax > 0, np.frexp(amax)[1] - 1 + 127 - 7, 1), 1, 254)
    codes = (b * np.exp2(127.0 - byte)[:, None, :]).reshape(n, m).astype(np.float32).astype(ml_dtypes.float8_e4m3fn).view(np.uint8)
    words = codes.reshape(n // 512, 128, 4, m).transpose(0, 1, 3, 2)
    return np.ascontiguousarray(words), np.ascontiguousarray(byte.astype(np.uint8).reshape(n // 512, 16, m))


K, H, N, K2, T, S, T2, P = 1536, 512, 1024, 1024, 4096, 1024, 2048, 512


def setup_inputs():
    n = np.random.standard_normal
    s = mx_kscale(K)[:, None]
    s2 = mx_kscale(K2)[:, None]
    u = mx_kscale(H)[:, None]
    size = np.exp(0.8 * n(N))[None, :]
    tab_words, tab_scales = pack_weight(n((K, T)) * s, "e4m3")
    tab2_words, tab2_scales = pack_weight(n((K2, T2)) * s2, "e4m3")
    w4_words, w4_scales = pack_weight(n((H, N)) * size / np.sqrt(H) / u, "e2m1")
    w8_words, w8_scales = pack_weight(n((K2, N)) * size / np.sqrt(K2) / s2, "e4m3")
    return {
        "tab_words": tab_words, "tab_scales": tab_scales,
        "offs": striped(np.random.permutation(T)[:S]),
        "tab2_words": tab2_words, "tab2_scales": tab2_scales,
        "offs2": striped(np.random.permutation(T2)[:P]),
        "pos1": striped(np.random.permutation(S)[:P]),
        "w1": (0.5 * n((K, H)) / np.sqrt(K) / s).astype(np.float32),
        "gain": (2.5 * np.exp(0.3 * n(H)) * u[:, 0]).astype(np.float32),
        "w4_words": w4_words, "w4_scales": w4_scales,
        "w8_words": w8_words, "w8_scales": w8_scales,
        "mat": n((N, P)).astype(np.float32),
    }


def reference(tab_words, tab_scales, offs, tab2_words, tab2_scales, offs2, pos1, w1, gain,
              w4_words, w4_scales, w8_words, w8_scales, mat):
    v = unpack_weight(tab_words, tab_scales, "e4m3")[:, unstriped(offs)]
    v2 = unpack_weight(tab2_words, tab2_scales, "e4m3")[:, unstriped(offs2)]
    a = mxq(f64(w1), 0, "e4m3").T @ v
    h = f64(gain)[:, None] * (a * np.cos(a))
    e = unpack_weight(w4_words, w4_scales, "e2m1").T @ mxq(h, 0, "e4m3")
    b = unpack_weight(w8_words, w8_scales, "e4m3").T @ v2
    y = e[:, unstriped(pos1)] + f64(mat) * b
    words, scales = planes(y)
    return y, words, scales

@@ -1,0 +1,245 @@
+import math
+from contextlib import ExitStack
+
+import concourse.mybir as mybir
+
+K, H, N, K2, T, S, T2, NP = 1536, 512, 1024, 1024, 4096, 1024, 2048, 512
+FLOPS = 2 * (K * H * S + H * N * S + K2 * N * NP)
+
+F32 = mybir.dt.float32
+BF16 = mybir.dt.bfloat16
+I32 = mybir.dt.int32
+U32 = mybir.dt.uint32
+U16 = mybir.dt.uint16
+U8 = mybir.dt.uint8
+FP8X4 = mybir.dt.float8_e4m3fn_x4
+FP4X4 = mybir.dt.float4_e2m1fn_x4
+ALU = mybir.AluOpType
+ACT = mybir.ActivationFunctionType
+
+P = 128
+PACK = 4
+K_PASS = P * PACK
+BANK = 512
+QUADS = 4
+LIST_ROWS = 16
+
+
+def tile_list_nailfold_vessel_scores_kernel(
+    tc, tab_words, tab_scales, offs, tab2_words, tab2_scales, offs2, pos1, w1, gain,
+    w4_words, w4_scales, w8_words, w8_scales, mat, out_0, out_1, out_2,
+):
+    nc = tc.nc
+    passes, passes2 = K // K_PASS, K2 // K_PASS
+    halves, groups = S // BANK, N // K_PASS
+
+    with ExitStack() as ctx:
+        lists = ctx.enter_context(tc.tile_pool(name="lists", bufs=1))
+        keep = ctx.enter_context(tc.tile_pool(name="keep", bufs=1))
+        ring = ctx.enter_context(tc.tile_pool(name="ring", bufs=1))
+        psum = ctx.enter_context(tc.psum_pool(name="psum", bufs=1))
+
+        def kept(name, shape, dtype):
+            return keep.tile(shape, dtype, name=name, align_bytes=64)
+
+        def bank(index):
+            return psum.tile([P, BANK], F32, name="bank%d" % index, tag="bank%d" % index)
+
+        def wide_f32(name):
+            return ring.tile([P, PACK, BANK], F32, name=name, tag="wide_f32", bufs=4, align_bytes=64)
+
+        def woven_bf16(name):
+            return ring.tile([P, PACK * BANK], BF16, name=name, tag="woven", bufs=3, align_bytes=64)
+
+        def load_words(name, dram_words):
+            words = kept(name, [P, dram_words.shape[1]], I32)
+            nc.sync.dma_start(out=words[:], in_=dram_words.rearrange("p n t -> p (n t)").bitcast(I32))
+            return words
+
+        def load_scale_rows(plane, first_row, dram_scales):
+            rows = PACK * dram_scales.shape[0]
+            for q in range(QUADS):
+                nc.gpsimd.dma_start(
+                    out=plane[32 * q + first_row : 32 * q + first_row + rows, :].bitcast(I32),
+                    in_=dram_scales[:, PACK * q : PACK * (q + 1), :].bitcast(I32),
+                )
+
+        def weave(engine_copy, woven, slices):
+            engine_copy(
+                out=woven[:].rearrange("p (c i t) -> p c t i", i=4, t=PACK),
+                in_=slices[:].rearrange("p t (c i) -> p c t i", i=4),
+            )
+
+        offs_sb = lists.tile([P, S // LIST_ROWS], U16, name="offs_sb")
+        offs2_sb = lists.tile([P, NP // LIST_ROWS], U16, name="offs2_sb")
+        pos1_sb = lists.tile([P, NP // LIST_ROWS], U16, name="pos1_sb")
+
+        tab_plane = kept("tab_plane", [P, T], U8)
+        tab2_plane = kept("tab2_plane", [P, T2], U8)
+        w_plane = kept("w_plane", [P, N], U8)
+        for plane in (tab_plane, w_plane, tab2_plane):
+            nc.vector.memset(plane[:].bitcast(I32), 0)
+        load_scale_rows(tab_plane, 0, tab_scales)
+        load_scale_rows(w_plane, 0, w4_scales)
+        load_scale_rows(w_plane, PACK, w8_scales)
+        load_scale_rows(tab2_plane, 0, tab2_scales)
+
+        def load_w1(a):
+            raw = wide_f32("w1_raw%d" % a)
+            nc.sync.dma_start(out=raw[:], in_=w1[a * K_PASS : (a + 1) * K_PASS, :].rearrange("(p j) c -> p j c", j=PACK))
+            return raw
+
+        w1_raw = [load_w1(0)]
+        nc.sync.dma_start(offs_sb[:], offs)
+        tab_sb = [load_words("tab_sb0", tab_words[0])]
+        w1_raw.append(load_w1(1))
+        w4_sb = kept("w4_sb", [P, 2 * N], U8)
+        nc.sync.dma_start(out=w4_sb[:].bitcast(I32), in_=w4_words[0].bitcast(I32))
+        nc.sync.dma_start(offs2_sb[:], offs2)
+        w1_raw.append(load_w1(2))
+        tab_sb.append(load_words("tab_sb1", tab_words[1]))
+        tab_sb.append(load_words("tab_sb2", tab_words[2]))
+        gain_sb = kept("gain_sb", [P, PACK], F32)
+        nc.sync.dma_start(out=gain_sb[:], in_=gain.rearrange("(p t) -> p t", t=PACK))
+        w8_sb = [load_words("w8_sb%d" % a, w8_words[a]) for a in range(passes2)]
+        tab2_sb = [load_words("tab2_sb%d" % a, tab2_words[a]) for a in range(passes2)]
+        nc.sync.dma_start(pos1_sb[:], pos1)
+        mat_rows = mat.rearrange("(g p t) j -> g p t j", p=P, t=PACK)
+        mat_sb = []
+        for g in range(groups):
+            mat_sb.append(kept("mat_sb%d" % g, [P, PACK, NP], F32))
+            nc.sync.dma_start(out=mat_sb[g][:], in_=mat_rows[g])
+
+        w1_codes, w1_planes = [], []
+
+        def quantise_w1(a):
+            woven = woven_bf16("w1_woven%d" % a)
+            nc.scalar.copy(
+                out=woven[:].rearrange("p (t m j) -> p m j t", t=PACK, j=PACK),
+                in_=w1_raw[a][:].rearrange("p j (m t) -> p m j t", t=PACK),
+            )
+            w1_codes.append(kept("w1_codes%d" % a, [P, H], U32))
+            w1_planes.append(kept("w1_plane%d" % a, [P, H], U8))
+            nc.vector.quantize_mx(out=w1_codes[a][:].bitcast(FP8X4), scales=w1_planes[a][:], in_=woven[:])
+
+        a_banks = [[bank(PACK * half + t) for t in range(PACK)] for half in range(halves)]
+        v_plane = kept("v_plane", [P, S], U8)
+        list_cols = BANK // LIST_ROWS
+
+        def first_stage_pass(a):
+            for half in range(halves):
+                picked = kept("v_words%d_%d" % (a, half), [P, BANK], U32)
+                nc.vector.tensor_copy(
+                    picked[:], tab_sb[a][:].bitcast(U32).indirect(offs_sb[:, half * list_cols : (half + 1) * list_cols])
+                )
+                for t in range(PACK):
+                    nc.tensor.matmul_mx(
+                        out=a_banks[half][t][:],
+                        lhsT=w1_codes[a][:, t * P : (t + 1) * P].bitcast(FP8X4),
+                        lhsT_scale=w1_planes[a][:, t * P : (t + 1) * P],
+                        rhs=picked[:].bitcast(FP8X4),
+                        rhs_scale=v_plane[PACK * a :, half * BANK : (half + 1) * BANK],
+                        start=(a == 0),
+                        stop=(a == passes - 1),
+                    )
+
+        quantise_w1(0)
+        nc.vector.tensor_copy(v_plane[:], tab_plane[:].indirect(offs_sb[:]))
+        first_stage_pass(0)
+        quantise_w1(1)
+
+        w4_dealt = kept("w4_dealt", [P, 2 * N], U8)
+        nc.vector.tensor_copy(
+            out=w4_dealt[:].rearrange("p (g t m b) -> p g m t b", g=groups, t=PACK, b=2),
+            in_=w4_sb[:].rearrange("p (g m t b) -> p g m t b", g=groups, t=PACK, b=2),
+        )
+        w_plane_dealt = kept("w_plane_dealt", [P, N], U8)
+        nc.vector.tensor_copy(
+            out=w_plane_dealt[:].rearrange("p (g t m) -> p g m t", g=groups, t=PACK),
+            in_=w_plane[:].rearrange("p (g m t) -> p g m t", g=groups, t=PACK),
+        )
+        v2_plane = kept("v2_plane", [P, NP], U8)
+        nc.vector.tensor_copy(v2_plane[:], tab2_plane[:].indirect(offs2_sb[:]))
+
+        quantise_w1(2)
+        first_stage_pass(1)
+        first_stage_pass(2)
+
+        h_codes = [kept("h_codes%d" % half, [P, BANK], U32) for half in range(halves)]
+        h_planes = [kept("h_plane%d" % half, [P, BANK], U8) for half in range(halves)]
+        h_slices = []
+        for half in range(halves):
+            h_slices.append(wide_f32("h_slices%d" % half))
+            for t in range(PACK):
+                size = ring.tile([P, BANK], F32, name="size", bufs=2)
+                cosine = ring.tile([P, BANK], F32, name="cosine", bufs=3)
+                nc.scalar.activation(out=size[:], in_=a_banks[half][t][:], func=ACT.Abs)
+                nc.scalar.activation(out=cosine[:], in_=size[:], func=ACT.Sin, scale=-1.0, bias=math.pi / 2)
+                nc.vector.scalar_tensor_tensor(
+                    out=h_slices[half][:, t, :], in0=a_banks[half][t][:], scalar=gain_sb[:, t : t + 1], in1=cosine[:],
+                    op0=ALU.mult, op1=ALU.mult,
+                )
+        for half in range(halves):
+            woven = woven_bf16("h_woven%d" % half)
+            weave(nc.scalar.copy, woven, h_slices[half])
+            nc.vector.quantize_mx(out=h_codes[half][:].bitcast(FP8X4), scales=h_planes[half][:], in_=woven[:])
+
+        w8_dealt, v2_words = [], []
+        for a in range(passes2):
+            w8_dealt.append(kept("w8_dealt%d" % a, [P, N], I32))
+            nc.vector.tensor_copy(
+                out=w8_dealt[a][:].rearrange("p (g t m) -> p g m t", g=groups, t=PACK),
+                in_=w8_sb[a][:].rearrange("p (g m t) -> p g m t", g=groups, t=PACK),
+            )
+        for a in range(passes2):
+            v2_words.append(kept("v2_words%d" % a, [P, NP], U32))
+            nc.vector.tensor_copy(v2_words[a][:], tab2_sb[a][:].bitcast(U32).indirect(offs2_sb[:]))
+        for g in range(groups):
+            for t in range(PACK):
+                s = PACK * g + t
+                cols = slice(s * P, (s + 1) * P)
+                b_bank = bank(s % 3)
+                for a in range(passes2):
+                    nc.tensor.matmul_mx(
+                        out=b_bank[:],
+                        lhsT=w8_dealt[a][:, cols].bitcast(FP8X4),
+                        lhsT_scale=w_plane_dealt[PACK * (a + 1) :, cols],
+                        rhs=v2_words[a][:].bitcast(FP8X4),
+                        rhs_scale=v2_plane[PACK * a :, :],
+                        start=(a == 0),
+                        stop=(a == passes2 - 1),
+                    )
+                nc.vector.tensor_tensor(out=mat_sb[g][:, t, :], in0=b_bank[:], in1=mat_sb[g][:, t, :], op=ALU.mult)
+
+        y_rows = out_0.rearrange("(g p t) j -> g p t j", p=P, t=PACK)
+        y_plane = kept("y_plane", [P, groups, NP], U8)
+        for g in range(groups):
+            y_slices = wide_f32("y_slices%d" % g)
+            for t in range(PACK):
+                s = PACK * g + t
+                e_rows = ring.tile([P, S], F32, name="e_rows", bufs=6)
+                for half in range(halves):
+                    e_bank = bank(3 + (halves * s + half) % 5)
+                    nc.tensor.matmul_mx(
+                        out=e_bank[:],
+                        lhsT=w4_dealt[:, 2 * s * P : 2 * (s + 1) * P].bitcast(FP4X4),
+                        lhsT_scale=w_plane_dealt[:, s * P : (s + 1) * P],
+                        rhs=h_codes[half][:].bitcast(FP8X4),
+                        rhs_scale=h_planes[half][:],
+                        start=True,
+                        stop=True,
+                    )
+                    nc.scalar.copy(out=e_rows[:, half * BANK : (half + 1) * BANK], in_=e_bank[:])
+                nc.vector.tensor_tensor(y_slices[:, t, :], e_rows[:].indirect(pos1_sb[:]), mat_sb[g][:, t, :], ALU.add)
+                nc.sync.dma_start(out=y_rows[g][:, t, :], in_=y_slices[:, t, :])
+            woven = woven_bf16("y_woven%d" % g)
+            weave(nc.scalar.copy if g < groups - 1 else nc.vector.tensor_copy, woven, y_slices)
+            y_codes = kept("y_codes%d" % g, [P, NP], I32)
+            nc.vector.quantize_mx(out=y_codes[:].bitcast(FP8X4), scales=y_plane[:, g, :], in_=woven[:])
+            nc.sync.dma_start(out=out_1[g].rearrange("p m t -> p (m t)").bitcast(I32), in_=y_codes[:])
+        for q in range(QUADS):
+            queue = nc.scalar if q % 2 == 0 else nc.sync
+            queue.dma_start(
+                out=out_2[:, PACK * q : PACK * (q + 1), :].rearrange("g r m -> r g m").bitcast(I32),
+                in_=y_plane[32 * q : 32 * q + PACK, :, :].bitcast(I32),
+            )

@@ -23,6 +23,7 @@ K_PASS = P * PACK
 BANK = 512
 QUADS = 4
 LIST_ROWS = 16
+SCALAR_SHARE = 176
 
 
 def tile_list_nailfold_vessel_scores_kernel(
@@ -39,35 +40,39 @@ def tile_list_nailfold_vessel_scores_kernel(
         ring = ctx.enter_context(tc.tile_pool(name="ring", bufs=1))
         psum = ctx.enter_context(tc.psum_pool(name="psum", bufs=1))
 
-        def kept(name, shape, dtype):
-            return keep.tile(shape, dtype, name=name, align_bytes=64)
+        def kept(name, shape, dtype, over=None):
+            return keep.tile(shape, dtype, name=name, tag=over or name, align_bytes=64)
 
         def bank(index):
             return psum.tile([P, BANK], F32, name="bank%d" % index, tag="bank%d" % index)
 
         def wide_f32(name):
-            return ring.tile([P, PACK, BANK], F32, name=name, tag="wide_f32", bufs=4, align_bytes=64)
+            return ring.tile([P, PACK, BANK], F32, name=name, tag="wide_f32", bufs=3, align_bytes=64)
 
         def woven_bf16(name):
             return ring.tile([P, PACK * BANK], BF16, name=name, tag="woven", bufs=3, align_bytes=64)
 
-        def load_words(name, dram_words):
-            words = kept(name, [P, dram_words.shape[1]], I32)
-            nc.sync.dma_start(out=words[:], in_=dram_words.rearrange("p n t -> p (n t)").bitcast(I32))
+        def load_words(name, dram_words, pieces=1):
+            width = dram_words.shape[1]
+            words = kept(name, [P, width], I32)
+            flat = dram_words.rearrange("p n t -> p (n t)").bitcast(I32)
+            for piece in range(pieces):
+                cols = slice(piece * width // pieces, (piece + 1) * width // pieces)
+                nc.sync.dma_start(out=words[:, cols], in_=flat[:, cols])
             return words
 
-        def load_scale_rows(plane, first_row, dram_scales):
+        def load_scale_rows(plane, first_row, dram_scales, quads):
             rows = PACK * dram_scales.shape[0]
-            for q in range(QUADS):
-                nc.gpsimd.dma_start(
+            for q in quads:
+                nc.sync.dma_start(
                     out=plane[32 * q + first_row : 32 * q + first_row + rows, :].bitcast(I32),
                     in_=dram_scales[:, PACK * q : PACK * (q + 1), :].bitcast(I32),
                 )
 
         def weave(engine_copy, woven, slices):
             engine_copy(
-                out=woven[:].rearrange("p (c i t) -> p c t i", i=4, t=PACK),
-                in_=slices[:].rearrange("p t (c i) -> p c t i", i=4),
+                out=woven.rearrange("p (c i t) -> p c t i", i=4, t=PACK),
+                in_=slices.rearrange("p t (c i) -> p c t i", i=4),
             )
 
         offs_sb = lists.tile([P, S // LIST_ROWS], U16, name="offs_sb")
@@ -79,45 +84,69 @@ def tile_list_nailfold_vessel_scores_kernel(
         w_plane = kept("w_plane", [P, N], U8)
         for plane in (tab_plane, w_plane, tab2_plane):
             nc.vector.memset(plane[:].bitcast(I32), 0)
-        load_scale_rows(tab_plane, 0, tab_scales)
-        load_scale_rows(w_plane, 0, w4_scales)
-        load_scale_rows(w_plane, PACK, w8_scales)
-        load_scale_rows(tab2_plane, 0, tab2_scales)
 
         def load_w1(a):
             raw = wide_f32("w1_raw%d" % a)
-            nc.sync.dma_start(out=raw[:], in_=w1[a * K_PASS : (a + 1) * K_PASS, :].rearrange("(p j) c -> p j c", j=PACK))
+            rows = w1[a * K_PASS : (a + 1) * K_PASS, :].rearrange("(p j) c -> p j c", j=PACK)
+            nc.sync.dma_start(out=raw[:], in_=rows)
             return raw
 
-        w1_raw = [load_w1(0)]
+        tab_sb = [load_words("tab_sb0", tab_words[0], pieces=2)]
         nc.sync.dma_start(offs_sb[:], offs)
-        tab_sb = [load_words("tab_sb0", tab_words[0])]
-        w1_raw.append(load_w1(1))
-        w4_sb = kept("w4_sb", [P, 2 * N], U8)
-        nc.sync.dma_start(out=w4_sb[:].bitcast(I32), in_=w4_words[0].bitcast(I32))
         nc.sync.dma_start(offs2_sb[:], offs2)
-        w1_raw.append(load_w1(2))
-        tab_sb.append(load_words("tab_sb1", tab_words[1]))
-        tab_sb.append(load_words("tab_sb2", tab_words[2]))
+        nc.sync.dma_start(pos1_sb[:], pos1)
         gain_sb = kept("gain_sb", [P, PACK], F32)
         nc.sync.dma_start(out=gain_sb[:], in_=gain.rearrange("(p t) -> p t", t=PACK))
-        w8_sb = [load_words("w8_sb%d" % a, w8_words[a]) for a in range(passes2)]
-        tab2_sb = [load_words("tab2_sb%d" % a, tab2_words[a]) for a in range(passes2)]
-        nc.sync.dma_start(pos1_sb[:], pos1)
+        w1_raw = [load_w1(0)]
+        w4_sb = kept("w4_sb", [P, 2 * N], U8)
+        nc.sync.dma_start(out=w4_sb[:].bitcast(I32), in_=w4_words[0].bitcast(I32))
+        load_scale_rows(tab_plane, 0, tab_scales, range(QUADS))
+        tab_sb.append(load_words("tab_sb1", tab_words[1]))
+        w1_raw.append(load_w1(1))
+        load_scale_rows(w_plane, 0, w4_scales, (0, 1))
+        tab_sb.append(load_words("tab_sb2", tab_words[2]))
+        w1_raw.append(load_w1(2))
         mat_rows = mat.rearrange("(g p t) j -> g p t j", p=P, t=PACK)
-        mat_sb = []
-        for g in range(groups):
-            mat_sb.append(kept("mat_sb%d" % g, [P, PACK, NP], F32))
-            nc.sync.dma_start(out=mat_sb[g][:], in_=mat_rows[g])
+
+        def load_w8(g):
+            words = kept("w8_sb%d" % g, [P, passes2, K_PASS], I32)
+            group = w8_words[:, :, g * K_PASS : (g + 1) * K_PASS, :]
+            nc.sync.dma_start(out=words[:], in_=group.rearrange("a p n t -> p a (n t)").bitcast(I32))
+            return words
+
+        def load_mat(g):
+            rows = kept("mat_sb%d" % g, [P, PACK, NP], F32)
+            nc.sync.dma_start(out=rows[:], in_=mat_rows[g])
+            return rows
+
+        load_scale_rows(tab2_plane, 0, tab2_scales, (0, 1, 2))
+        tab2_sb = [load_words("tab2_sb0", tab2_words[0])]
+        load_scale_rows(tab2_plane, 0, tab2_scales, (3,))
+        load_scale_rows(w_plane, 0, w4_scales, (2, 3))
+        tab2_sb.append(load_words("tab2_sb1", tab2_words[1]))
+        load_scale_rows(w_plane, PACK, w8_scales, range(QUADS))
+        w8_sb = [load_w8(0)]
+        mat_sb = [load_mat(0)]
+        w8_sb.append(load_w8(1))
+        mat_sb.append(load_mat(1))
+
+        def deal_plane(name, plane):
+            dealt = kept(name, [P, N], U8)
+            nc.vector.tensor_copy(
+                out=dealt[:].rearrange("p (g t m) -> p g m t", g=groups, t=PACK),
+                in_=plane[:].rearrange("p (g m t) -> p g m t", g=groups, t=PACK),
+            )
+            return dealt
 
         w1_codes, w1_planes = [], []
 
-        def quantise_w1(a):
+        def quantise_w1(a, shares):
             woven = woven_bf16("w1_woven%d" % a)
-            nc.scalar.copy(
-                out=woven[:].rearrange("p (t m j) -> p m j t", t=PACK, j=PACK),
-                in_=w1_raw[a][:].rearrange("p j (m t) -> p m j t", t=PACK),
-            )
+            dealt = woven[:].rearrange("p (t m j) -> p m j t", t=PACK, j=PACK)
+            natural = w1_raw[a][:].rearrange("p j (m t) -> p m j t", t=PACK)
+            for engine_copy, cols in shares:
+                ms = slice(cols.start // PACK, cols.stop // PACK)
+                engine_copy(out=dealt[:, ms, :, :], in_=natural[:, ms, :, :])
             w1_codes.append(kept("w1_codes%d" % a, [P, H], U32))
             w1_planes.append(kept("w1_plane%d" % a, [P, H], U8))
             nc.vector.quantize_mx(out=w1_codes[a][:].bitcast(FP8X4), scales=w1_planes[a][:], in_=woven[:])
@@ -126,117 +155,155 @@ def tile_list_nailfold_vessel_scores_kernel(
         v_plane = kept("v_plane", [P, S], U8)
         list_cols = BANK // LIST_ROWS
 
-        def first_stage_pass(a):
+        def pick_table(a):
+            picked = []
             for half in range(halves):
-                picked = kept("v_words%d_%d" % (a, half), [P, BANK], U32)
+                picked.append(kept("v_words%d_%d" % (a, half), [P, BANK], U32))
                 nc.vector.tensor_copy(
-                    picked[:], tab_sb[a][:].bitcast(U32).indirect(offs_sb[:, half * list_cols : (half + 1) * list_cols])
+                    picked[half][:],
+                    tab_sb[a][:].bitcast(U32).indirect(offs_sb[:, half * list_cols : (half + 1) * list_cols]),
                 )
+            return picked
+
+        def first_stage_pass(a, picked):
+            for half in range(halves):
                 for t in range(PACK):
                     nc.tensor.matmul_mx(
                         out=a_banks[half][t][:],
                         lhsT=w1_codes[a][:, t * P : (t + 1) * P].bitcast(FP8X4),
                         lhsT_scale=w1_planes[a][:, t * P : (t + 1) * P],
-                        rhs=picked[:].bitcast(FP8X4),
+                        rhs=picked[half][:].bitcast(FP8X4),
                         rhs_scale=v_plane[PACK * a :, half * BANK : (half + 1) * BANK],
                         start=(a == 0),
                         stop=(a == passes - 1),
                     )
 
-        quantise_w1(0)
-        nc.vector.tensor_copy(v_plane[:], tab_plane[:].indirect(offs_sb[:]))
-        first_stage_pass(0)
-        quantise_w1(1)
+        picked = pick_table(0)
+        quantise_w1(0, [(nc.scalar.copy, slice(0, H))])
 
         w4_dealt = kept("w4_dealt", [P, 2 * N], U8)
         nc.vector.tensor_copy(
             out=w4_dealt[:].rearrange("p (g t m b) -> p g m t b", g=groups, t=PACK, b=2),
             in_=w4_sb[:].rearrange("p (g m t b) -> p g m t b", g=groups, t=PACK, b=2),
         )
-        w_plane_dealt = kept("w_plane_dealt", [P, N], U8)
-        nc.vector.tensor_copy(
-            out=w_plane_dealt[:].rearrange("p (g t m) -> p g m t", g=groups, t=PACK),
-            in_=w_plane[:].rearrange("p (g m t) -> p g m t", g=groups, t=PACK),
-        )
-        v2_plane = kept("v2_plane", [P, NP], U8)
-        nc.vector.tensor_copy(v2_plane[:], tab2_plane[:].indirect(offs2_sb[:]))
+        nc.vector.tensor_copy(v_plane[:], tab_plane[:].indirect(offs_sb[:]))
+        first_stage_pass(0, picked)
+        picked_1 = pick_table(1)
+        quantise_w1(1, [(nc.scalar.copy, slice(0, H))])
+        first_stage_pass(1, picked_1)
+        picked_2 = pick_table(2)
+        quantise_w1(2, [(nc.scalar.copy, slice(0, SCALAR_SHARE)), (nc.vector.tensor_copy, slice(SCALAR_SHARE, H))])
+        first_stage_pass(2, picked_2)
 
-        quantise_w1(2)
-        first_stage_pass(1)
-        first_stage_pass(2)
-
-        h_codes = [kept("h_codes%d" % half, [P, BANK], U32) for half in range(halves)]
         h_planes = [kept("h_plane%d" % half, [P, BANK], U8) for half in range(halves)]
-        h_slices = []
-        for half in range(halves):
-            h_slices.append(wide_f32("h_slices%d" % half))
+        sizes = kept("sizes", [P, 2, BANK], F32)
+
+        def gated_cosine(half, h_slices):
             for t in range(PACK):
-                size = ring.tile([P, BANK], F32, name="size", bufs=2)
-                cosine = ring.tile([P, BANK], F32, name="cosine", bufs=3)
-                nc.scalar.activation(out=size[:], in_=a_banks[half][t][:], func=ACT.Abs)
-                nc.scalar.activation(out=cosine[:], in_=size[:], func=ACT.Sin, scale=-1.0, bias=math.pi / 2)
+                size = sizes[:, t % 2, :]
+                cosine = ring.tile([P, BANK], F32, name="cosine", bufs=4)
+                nc.scalar.activation(out=size, in_=a_banks[half][t][:], func=ACT.Abs)
+                nc.scalar.activation(out=cosine[:], in_=size, func=ACT.Sin, scale=-1.0, bias=math.pi / 2)
                 nc.vector.scalar_tensor_tensor(
-                    out=h_slices[half][:, t, :], in0=a_banks[half][t][:], scalar=gain_sb[:, t : t + 1], in1=cosine[:],
+                    out=h_slices[:, t, :], in0=a_banks[half][t][:], scalar=gain_sb[:, t : t + 1], in1=cosine[:],
                     op0=ALU.mult, op1=ALU.mult,
                 )
-        for half in range(halves):
-            woven = woven_bf16("h_woven%d" % half)
-            weave(nc.scalar.copy, woven, h_slices[half])
-            nc.vector.quantize_mx(out=h_codes[half][:].bitcast(FP8X4), scales=h_planes[half][:], in_=woven[:])
 
-        w8_dealt, v2_words = [], []
-        for a in range(passes2):
-            w8_dealt.append(kept("w8_dealt%d" % a, [P, N], I32))
+        def quantise_h(half, woven, over):
+            codes = kept("h_codes%d" % half, [P, BANK], U32, over)
+            nc.vector.quantize_mx(out=codes[:].bitcast(FP8X4), scales=h_planes[half][:], in_=woven)
+            return codes
+
+        def deal_w8(g):
+            dealt = kept("w8_dealt%d" % g, [P, passes2, K_PASS], I32)
             nc.vector.tensor_copy(
-                out=w8_dealt[a][:].rearrange("p (g t m) -> p g m t", g=groups, t=PACK),
-                in_=w8_sb[a][:].rearrange("p (g m t) -> p g m t", g=groups, t=PACK),
+                out=dealt[:].rearrange("p a (t m) -> p a m t", t=PACK),
+                in_=w8_sb[g][:].rearrange("p a (m t) -> p a m t", t=PACK),
             )
-        for a in range(passes2):
-            v2_words.append(kept("v2_words%d" % a, [P, NP], U32))
-            nc.vector.tensor_copy(v2_words[a][:], tab2_sb[a][:].bitcast(U32).indirect(offs2_sb[:]))
-        for g in range(groups):
+            return dealt
+
+        def curve_products(g, w8_dealt, products):
             for t in range(PACK):
                 s = PACK * g + t
-                cols = slice(s * P, (s + 1) * P)
-                b_bank = bank(s % 3)
+                b_bank = bank(t)
                 for a in range(passes2):
                     nc.tensor.matmul_mx(
                         out=b_bank[:],
-                        lhsT=w8_dealt[a][:, cols].bitcast(FP8X4),
-                        lhsT_scale=w_plane_dealt[PACK * (a + 1) :, cols],
+                        lhsT=w8_dealt[:, a, t * P : (t + 1) * P].bitcast(FP8X4),
+                        lhsT_scale=w_plane_dealt[PACK * (a + 1) :, s * P : (s + 1) * P],
                         rhs=v2_words[a][:].bitcast(FP8X4),
                         rhs_scale=v2_plane[PACK * a :, :],
                         start=(a == 0),
                         stop=(a == passes2 - 1),
                     )
-                nc.vector.tensor_tensor(out=mat_sb[g][:, t, :], in0=b_bank[:], in1=mat_sb[g][:, t, :], op=ALU.mult)
+                nc.vector.tensor_tensor(out=products[:, t, :], in0=b_bank[:], in1=mat_sb[g][:, t, :], op=ALU.mult)
+
+        v2_plane = kept("v2_plane", [P, NP], U8)
+        nc.vector.tensor_copy(v2_plane[:], tab2_plane[:].indirect(offs2_sb[:]))
+        v2_words = []
+        for a in range(passes2):
+            v2_words.append(kept("v2_words%d" % a, [P, NP], U32))
+            nc.vector.tensor_copy(v2_words[a][:], tab2_sb[a][:].bitcast(U32).indirect(offs2_sb[:]))
+        h_first = kept("h_first", [P, PACK, BANK], F32, over="tab2_sb0")
+        gated_cosine(0, h_first)
+        w_plane_dealt = deal_plane("w_plane_dealt", w_plane)
+        w8_first = deal_w8(0)
+        h_second = kept("h_second", [P, PACK, BANK], F32, over="w8_sb0")
+        products = [wide_f32("products0"), mat_sb[1]]
+        gated_cosine(1, h_second)
+        woven_first = sizes[:].rearrange("p s c -> p (s c)").bitcast(BF16)
+        weave(nc.scalar.copy, woven_first, h_first[:])
+        woven_second = woven_bf16("woven_second")
+        weave(nc.vector.tensor_copy, woven_second[:, : 2 * BANK], h_second[:, :, : BANK // 2])
+        weave(nc.scalar.copy, woven_second[:, 2 * BANK :], h_second[:, :, BANK // 2 :])
+        curve_products(0, w8_first, products[0])
+        h_codes = [quantise_h(0, woven_first, "mat_sb0"), quantise_h(1, woven_second[:], None)]
+        curve_products(1, deal_w8(1), products[1])
 
         y_rows = out_0.rearrange("(g p t) j -> g p t j", p=P, t=PACK)
         y_plane = kept("y_plane", [P, groups, NP], U8)
-        for g in range(groups):
-            y_slices = wide_f32("y_slices%d" % g)
+
+        def second_stage_rows(s):
+            e_rows = ring.tile([P, S], F32, name="e_rows", bufs=8)
+            for half in range(halves):
+                e_bank = bank(PACK + (halves * s + half) % PACK)
+                nc.tensor.matmul_mx(
+                    out=e_bank[:],
+                    lhsT=w4_dealt[:, 2 * s * P : 2 * (s + 1) * P].bitcast(FP4X4),
+                    lhsT_scale=w_plane_dealt[:, s * P : (s + 1) * P],
+                    rhs=h_codes[half][:].bitcast(FP8X4),
+                    rhs_scale=h_planes[half][:],
+                    start=True,
+                    stop=True,
+                )
+                nc.scalar.copy(out=e_rows[:, half * BANK : (half + 1) * BANK], in_=e_bank[:])
+            return e_rows
+
+        def pick_and_add(y_slices, e_rows, g, t, cols):
+            picks = pos1_sb[:, cols.start // LIST_ROWS : cols.stop // LIST_ROWS]
+            nc.vector.tensor_tensor(y_slices[:, t, cols], e_rows[:].indirect(picks), products[g][:, t, cols], ALU.add)
+
+        def quantise_y(engine_copy, y_slices, g, cols):
+            width = cols.stop - cols.start
+            woven = woven_bf16("y_woven%d_%d" % (g, cols.start))
+            weave(engine_copy, woven[:, : PACK * width], y_slices[:, :, cols])
+            y_codes = kept("y_codes%d_%d" % (g, cols.start), [P, width], I32)
+            nc.vector.quantize_mx(out=y_codes[:].bitcast(FP8X4), scales=y_plane[:, g, cols], in_=woven[:, : PACK * width])
+            nc.sync.dma_start(out=out_1[g][:, cols, :].rearrange("p m t -> p (m t)").bitcast(I32), in_=y_codes[:])
+
+        whole = slice(0, NP)
+        y_first = kept("y_first", [P, PACK, NP], F32, over="w8_sb1")
+        for t in range(PACK):
+            pick_and_add(y_first, second_stage_rows(t), 0, t, whole)
+            nc.sync.dma_start(out=y_rows[0][:, t, :], in_=y_first[:, t, :])
+        e_last = [second_stage_rows(PACK + t) for t in range(PACK)]
+        quantise_y(nc.scalar.copy, y_first, 0, whole)
+        y_last = wide_f32("y_slices1")
+        for cols, engine_copy in ((slice(0, NP // 2), nc.scalar.copy), (slice(NP // 2, NP), nc.vector.tensor_copy)):
             for t in range(PACK):
-                s = PACK * g + t
-                e_rows = ring.tile([P, S], F32, name="e_rows", bufs=6)
-                for half in range(halves):
-                    e_bank = bank(3 + (halves * s + half) % 5)
-                    nc.tensor.matmul_mx(
-                        out=e_bank[:],
-                        lhsT=w4_dealt[:, 2 * s * P : 2 * (s + 1) * P].bitcast(FP4X4),
-                        lhsT_scale=w_plane_dealt[:, s * P : (s + 1) * P],
-                        rhs=h_codes[half][:].bitcast(FP8X4),
-                        rhs_scale=h_planes[half][:],
-                        start=True,
-                        stop=True,
-                    )
-                    nc.scalar.copy(out=e_rows[:, half * BANK : (half + 1) * BANK], in_=e_bank[:])
-                nc.vector.tensor_tensor(y_slices[:, t, :], e_rows[:].indirect(pos1_sb[:]), mat_sb[g][:, t, :], ALU.add)
-                nc.sync.dma_start(out=y_rows[g][:, t, :], in_=y_slices[:, t, :])
-            woven = woven_bf16("y_woven%d" % g)
-            weave(nc.scalar.copy if g < groups - 1 else nc.vector.tensor_copy, woven, y_slices)
-            y_codes = kept("y_codes%d" % g, [P, NP], I32)
-            nc.vector.quantize_mx(out=y_codes[:].bitcast(FP8X4), scales=y_plane[:, g, :], in_=woven[:])
-            nc.sync.dma_start(out=out_1[g].rearrange("p m t -> p (m t)").bitcast(I32), in_=y_codes[:])
+                pick_and_add(y_last, e_last[t], 1, t, cols)
+            nc.sync.dma_start(out=y_rows[1][:, :, cols], in_=y_last[:, :, cols])
+            quantise_y(engine_copy, y_last, 1, cols)
         for q in range(QUADS):
             queue = nc.scalar if q % 2 == 0 else nc.sync
             queue.dma_start(

import math
from contextlib import ExitStack

import concourse.mybir as mybir

K, H, N, K2, T, S, T2, NP = 1536, 512, 1024, 1024, 4096, 1024, 2048, 512
FLOPS = 2 * (K * H * S + H * N * S + K2 * N * NP)

F32 = mybir.dt.float32
BF16 = mybir.dt.bfloat16
I32 = mybir.dt.int32
U32 = mybir.dt.uint32
U16 = mybir.dt.uint16
U8 = mybir.dt.uint8
FP8X4 = mybir.dt.float8_e4m3fn_x4
FP4X4 = mybir.dt.float4_e2m1fn_x4
ALU = mybir.AluOpType
ACT = mybir.ActivationFunctionType

P = 128
PACK = 4
K_PASS = P * PACK
BANK = 512
QUADS = 4
LIST_ROWS = 16
SCALAR_SHARE = 176


def tile_list_nailfold_vessel_scores_kernel(
    tc, tab_words, tab_scales, offs, tab2_words, tab2_scales, offs2, pos1, w1, gain,
    w4_words, w4_scales, w8_words, w8_scales, mat, out_0, out_1, out_2,
):
    nc = tc.nc
    passes, passes2 = K // K_PASS, K2 // K_PASS
    halves, groups = S // BANK, N // K_PASS

    with ExitStack() as ctx:
        lists = ctx.enter_context(tc.tile_pool(name="lists", bufs=1))
        keep = ctx.enter_context(tc.tile_pool(name="keep", bufs=1))
        ring = ctx.enter_context(tc.tile_pool(name="ring", bufs=1))
        psum = ctx.enter_context(tc.psum_pool(name="psum", bufs=1))

        def kept(name, shape, dtype, over=None):
            return keep.tile(shape, dtype, name=name, tag=over or name, align_bytes=64)

        def bank(index):
            return psum.tile([P, BANK], F32, name="bank%d" % index, tag="bank%d" % index)

        def wide_f32(name):
            return ring.tile([P, PACK, BANK], F32, name=name, tag="wide_f32", bufs=3, align_bytes=64)

        def woven_bf16(name):
            return ring.tile([P, PACK * BANK], BF16, name=name, tag="woven", bufs=3, align_bytes=64)

        def load_words(name, dram_words, pieces=1):
            width = dram_words.shape[1]
            words = kept(name, [P, width], I32)
            flat = dram_words.rearrange("p n t -> p (n t)").bitcast(I32)
            for piece in range(pieces):
                cols = slice(piece * width // pieces, (piece + 1) * width // pieces)
                nc.sync.dma_start(out=words[:, cols], in_=flat[:, cols])
            return words

        def load_scale_rows(plane, first_row, dram_scales, quads):
            rows = PACK * dram_scales.shape[0]
            for q in quads:
                nc.sync.dma_start(
                    out=plane[32 * q + first_row : 32 * q + first_row + rows, :].bitcast(I32),
                    in_=dram_scales[:, PACK * q : PACK * (q + 1), :].bitcast(I32),
                )

        def weave(engine_copy, woven, slices):
            engine_copy(
                out=woven.rearrange("p (c i t) -> p c t i", i=4, t=PACK),
                in_=slices.rearrange("p t (c i) -> p c t i", i=4),
            )

        offs_sb = lists.tile([P, S // LIST_ROWS], U16, name="offs_sb")
        offs2_sb = lists.tile([P, NP // LIST_ROWS], U16, name="offs2_sb")
        pos1_sb = lists.tile([P, NP // LIST_ROWS], U16, name="pos1_sb")

        tab_plane = kept("tab_plane", [P, T], U8)
        tab2_plane = kept("tab2_plane", [P, T2], U8)
        w_plane = kept("w_plane", [P, N], U8)
        for plane in (tab_plane, w_plane, tab2_plane):
            nc.vector.memset(plane[:].bitcast(I32), 0)

        def load_w1(a):
            raw = wide_f32("w1_raw%d" % a)
            rows = w1[a * K_PASS : (a + 1) * K_PASS, :].rearrange("(p j) c -> p j c", j=PACK)
            nc.sync.dma_start(out=raw[:], in_=rows)
            return raw

        tab_sb = [load_words("tab_sb0", tab_words[0], pieces=2)]
        nc.sync.dma_start(offs_sb[:], offs)
        nc.sync.dma_start(offs2_sb[:], offs2)
        nc.sync.dma_start(pos1_sb[:], pos1)
        gain_sb = kept("gain_sb", [P, PACK], F32)
        nc.sync.dma_start(out=gain_sb[:], in_=gain.rearrange("(p t) -> p t", t=PACK))
        w1_raw = [load_w1(0)]
        w4_sb = kept("w4_sb", [P, 2 * N], U8)
        nc.sync.dma_start(out=w4_sb[:].bitcast(I32), in_=w4_words[0].bitcast(I32))
        load_scale_rows(tab_plane, 0, tab_scales, range(QUADS))
        tab_sb.append(load_words("tab_sb1", tab_words[1]))
        w1_raw.append(load_w1(1))
        load_scale_rows(w_plane, 0, w4_scales, (0, 1))
        tab_sb.append(load_words("tab_sb2", tab_words[2]))
        w1_raw.append(load_w1(2))
        mat_rows = mat.rearrange("(g p t) j -> g p t j", p=P, t=PACK)

        def load_w8(g):
            words = kept("w8_sb%d" % g, [P, passes2, K_PASS], I32)
            group = w8_words[:, :, g * K_PASS : (g + 1) * K_PASS, :]
            nc.sync.dma_start(out=words[:], in_=group.rearrange("a p n t -> p a (n t)").bitcast(I32))
            return words

        def load_mat(g):
            rows = kept("mat_sb%d" % g, [P, PACK, NP], F32)
            nc.sync.dma_start(out=rows[:], in_=mat_rows[g])
            return rows

        load_scale_rows(tab2_plane, 0, tab2_scales, (0, 1, 2))
        tab2_sb = [load_words("tab2_sb0", tab2_words[0])]
        load_scale_rows(tab2_plane, 0, tab2_scales, (3,))
        load_scale_rows(w_plane, 0, w4_scales, (2, 3))
        tab2_sb.append(load_words("tab2_sb1", tab2_words[1]))
        load_scale_rows(w_plane, PACK, w8_scales, range(QUADS))
        w8_sb = [load_w8(0)]
        mat_sb = [load_mat(0)]
        w8_sb.append(load_w8(1))
        mat_sb.append(load_mat(1))

        def deal_plane(name, plane):
            dealt = kept(name, [P, N], U8)
            nc.vector.tensor_copy(
                out=dealt[:].rearrange("p (g t m) -> p g m t", g=groups, t=PACK),
                in_=plane[:].rearrange("p (g m t) -> p g m t", g=groups, t=PACK),
            )
            return dealt

        w1_codes, w1_planes = [], []

        def quantise_w1(a, shares):
            woven = woven_bf16("w1_woven%d" % a)
            dealt = woven[:].rearrange("p (t m j) -> p m j t", t=PACK, j=PACK)
            natural = w1_raw[a][:].rearrange("p j (m t) -> p m j t", t=PACK)
            for engine_copy, cols in shares:
                ms = slice(cols.start // PACK, cols.stop // PACK)
                engine_copy(out=dealt[:, ms, :, :], in_=natural[:, ms, :, :])
            w1_codes.append(kept("w1_codes%d" % a, [P, H], U32))
            w1_planes.append(kept("w1_plane%d" % a, [P, H], U8))
            nc.vector.quantize_mx(out=w1_codes[a][:].bitcast(FP8X4), scales=w1_planes[a][:], in_=woven[:])

        a_banks = [[bank(PACK * half + t) for t in range(PACK)] for half in range(halves)]
        v_plane = kept("v_plane", [P, S], U8)
        list_cols = BANK // LIST_ROWS

        def pick_table(a):
            picked = []
            for half in range(halves):
                picked.append(kept("v_words%d_%d" % (a, half), [P, BANK], U32))
                nc.vector.tensor_copy(
                    picked[half][:],
                    tab_sb[a][:].bitcast(U32).indirect(offs_sb[:, half * list_cols : (half + 1) * list_cols]),
                )
            return picked

        def first_stage_pass(a, picked):
            for half in range(halves):
                for t in range(PACK):
                    nc.tensor.matmul_mx(
                        out=a_banks[half][t][:],
                        lhsT=w1_codes[a][:, t * P : (t + 1) * P].bitcast(FP8X4),
                        lhsT_scale=w1_planes[a][:, t * P : (t + 1) * P],
                        rhs=picked[half][:].bitcast(FP8X4),
                        rhs_scale=v_plane[PACK * a :, half * BANK : (half + 1) * BANK],
                        start=(a == 0),
                        stop=(a == passes - 1),
                    )

        picked = pick_table(0)
        quantise_w1(0, [(nc.scalar.copy, slice(0, H))])

        w4_dealt = kept("w4_dealt", [P, 2 * N], U8)
        nc.vector.tensor_copy(
            out=w4_dealt[:].rearrange("p (g t m b) -> p g m t b", g=groups, t=PACK, b=2),
            in_=w4_sb[:].rearrange("p (g m t b) -> p g m t b", g=groups, t=PACK, b=2),
        )
        nc.vector.tensor_copy(v_plane[:], tab_plane[:].indirect(offs_sb[:]))
        first_stage_pass(0, picked)
        picked_1 = pick_table(1)
        quantise_w1(1, [(nc.scalar.copy, slice(0, H))])
        first_stage_pass(1, picked_1)
        picked_2 = pick_table(2)
        quantise_w1(2, [(nc.scalar.copy, slice(0, SCALAR_SHARE)), (nc.vector.tensor_copy, slice(SCALAR_SHARE, H))])
        first_stage_pass(2, picked_2)

        h_planes = [kept("h_plane%d" % half, [P, BANK], U8) for half in range(halves)]
        sizes = kept("sizes", [P, 2, BANK], F32)

        def gated_cosine(half, h_slices):
            for t in range(PACK):
                size = sizes[:, t % 2, :]
                cosine = ring.tile([P, BANK], F32, name="cosine", bufs=4)
                nc.scalar.activation(out=size, in_=a_banks[half][t][:], func=ACT.Abs)
                nc.scalar.activation(out=cosine[:], in_=size, func=ACT.Sin, scale=-1.0, bias=math.pi / 2)
                nc.vector.scalar_tensor_tensor(
                    out=h_slices[:, t, :], in0=a_banks[half][t][:], scalar=gain_sb[:, t : t + 1], in1=cosine[:],
                    op0=ALU.mult, op1=ALU.mult,
                )

        def quantise_h(half, woven, over):
            codes = kept("h_codes%d" % half, [P, BANK], U32, over)
            nc.vector.quantize_mx(out=codes[:].bitcast(FP8X4), scales=h_planes[half][:], in_=woven)
            return codes

        def deal_w8(g):
            dealt = kept("w8_dealt%d" % g, [P, passes2, K_PASS], I32)
            nc.vector.tensor_copy(
                out=dealt[:].rearrange("p a (t m) -> p a m t", t=PACK),
                in_=w8_sb[g][:].rearrange("p a (m t) -> p a m t", t=PACK),
            )
            return dealt

        def curve_products(g, w8_dealt, products):
            for t in range(PACK):
                s = PACK * g + t
                b_bank = bank(t)
                for a in range(passes2):
                    nc.tensor.matmul_mx(
                        out=b_bank[:],
                        lhsT=w8_dealt[:, a, t * P : (t + 1) * P].bitcast(FP8X4),
                        lhsT_scale=w_plane_dealt[PACK * (a + 1) :, s * P : (s + 1) * P],
                        rhs=v2_words[a][:].bitcast(FP8X4),
                        rhs_scale=v2_plane[PACK * a :, :],
                        start=(a == 0),
                        stop=(a == passes2 - 1),
                    )
                nc.vector.tensor_tensor(out=products[:, t, :], in0=b_bank[:], in1=mat_sb[g][:, t, :], op=ALU.mult)

        v2_plane = kept("v2_plane", [P, NP], U8)
        nc.vector.tensor_copy(v2_plane[:], tab2_plane[:].indirect(offs2_sb[:]))
        v2_words = []
        for a in range(passes2):
            v2_words.append(kept("v2_words%d" % a, [P, NP], U32))
            nc.vector.tensor_copy(v2_words[a][:], tab2_sb[a][:].bitcast(U32).indirect(offs2_sb[:]))
        h_first = kept("h_first", [P, PACK, BANK], F32, over="tab2_sb0")
        gated_cosine(0, h_first)
        w_plane_dealt = deal_plane("w_plane_dealt", w_plane)
        w8_first = deal_w8(0)
        h_second = kept("h_second", [P, PACK, BANK], F32, over="w8_sb0")
        products = [wide_f32("products0"), mat_sb[1]]
        gated_cosine(1, h_second)
        woven_first = sizes[:].rearrange("p s c -> p (s c)").bitcast(BF16)
        weave(nc.scalar.copy, woven_first, h_first[:])
        woven_second = woven_bf16("woven_second")
        weave(nc.vector.tensor_copy, woven_second[:, : 2 * BANK], h_second[:, :, : BANK // 2])
        weave(nc.scalar.copy, woven_second[:, 2 * BANK :], h_second[:, :, BANK // 2 :])
        curve_products(0, w8_first, products[0])
        h_codes = [quantise_h(0, woven_first, "mat_sb0"), quantise_h(1, woven_second[:], None)]
        curve_products(1, deal_w8(1), products[1])

        y_rows = out_0.rearrange("(g p t) j -> g p t j", p=P, t=PACK)
        y_plane = kept("y_plane", [P, groups, NP], U8)

        def second_stage_rows(s):
            e_rows = ring.tile([P, S], F32, name="e_rows", bufs=8)
            for half in range(halves):
                e_bank = bank(PACK + (halves * s + half) % PACK)
                nc.tensor.matmul_mx(
                    out=e_bank[:],
                    lhsT=w4_dealt[:, 2 * s * P : 2 * (s + 1) * P].bitcast(FP4X4),
                    lhsT_scale=w_plane_dealt[:, s * P : (s + 1) * P],
                    rhs=h_codes[half][:].bitcast(FP8X4),
                    rhs_scale=h_planes[half][:],
                    start=True,
                    stop=True,
                )
                nc.scalar.copy(out=e_rows[:, half * BANK : (half + 1) * BANK], in_=e_bank[:])
            return e_rows

        def pick_and_add(y_slices, e_rows, g, t, cols):
            picks = pos1_sb[:, cols.start // LIST_ROWS : cols.stop // LIST_ROWS]
            nc.vector.tensor_tensor(y_slices[:, t, cols], e_rows[:].indirect(picks), products[g][:, t, cols], ALU.add)

        def quantise_y(engine_copy, y_slices, g, cols):
            width = cols.stop - cols.start
            woven = woven_bf16("y_woven%d_%d" % (g, cols.start))
            weave(engine_copy, woven[:, : PACK * width], y_slices[:, :, cols])
            y_codes = kept("y_codes%d_%d" % (g, cols.start), [P, width], I32)
            nc.vector.quantize_mx(out=y_codes[:].bitcast(FP8X4), scales=y_plane[:, g, cols], in_=woven[:, : PACK * width])
            nc.sync.dma_start(out=out_1[g][:, cols, :].rearrange("p m t -> p (m t)").bitcast(I32), in_=y_codes[:])

        whole = slice(0, NP)
        y_first = kept("y_first", [P, PACK, NP], F32, over="w8_sb1")
        for t in range(PACK):
            pick_and_add(y_first, second_stage_rows(t), 0, t, whole)
            nc.sync.dma_start(out=y_rows[0][:, t, :], in_=y_first[:, t, :])
        e_last = [second_stage_rows(PACK + t) for t in range(PACK)]
        quantise_y(nc.scalar.copy, y_first, 0, whole)
        y_last = wide_f32("y_slices1")
        for cols, engine_copy in ((slice(0, NP // 2), nc.scalar.copy), (slice(NP // 2, NP), nc.vector.tensor_copy)):
            for t in range(PACK):
                pick_and_add(y_last, e_last[t], 1, t, cols)
            nc.sync.dma_start(out=y_rows[1][:, :, cols], in_=y_last[:, :, cols])
            quantise_y(engine_copy, y_last, 1, cols)
        for q in range(QUADS):
            queue = nc.scalar if q % 2 == 0 else nc.sync
            queue.dma_start(
                out=out_2[:, PACK * q : PACK * (q + 1), :].rearrange("g r m -> r g m").bitcast(I32),
                in_=y_plane[32 * q : 32 * q + PACK, :, :].bitcast(I32),
            )
